import numpy as np
import ml_dtypes


def mxq(x, axis, fmt="e4m3"):
    dtype, down = {"e4m3": (ml_dtypes.float8_e4m3fn, 7), "e5m2": (ml_dtypes.float8_e5m2, 14)}[fmt]
    v = np.moveaxis(np.asarray(x, np.float32).astype(ml_dtypes.bfloat16).astype(np.float64), axis, -1)
    blocks = v.reshape(v.shape[:-1] + (-1, 32))
    amax = np.abs(blocks).max(-1, keepdims=True)
    byte = np.maximum(np.where(amax > 0, np.frexp(amax)[1] - 1 + 127, 0) - down, 1)
    scale = np.exp2(byte - 127.0)
    codes = (blocks / scale).astype(np.float32).astype(dtype).astype(np.float64)
    return np.moveaxis((codes * scale).reshape(v.shape), -1, axis)


WIDE = False


def mx_kscale(k):
    if not WIDE:
        return np.ones(k)
    levels = np.array([10, -10, 5, -5, 0])
    if k % 512:
        return np.exp2(np.random.permutation(np.resize(levels, k // 32))).repeat(32)
    a = np.empty((k // 512, 16))
    for p in range(k // 512):
        a[p, :8] = np.random.permutation(np.resize(levels, 8))
        for g in range(8):
            far = levels[np.abs(levels - a[p, g]) >= 10]
            a[p, g + 8] = far[np.random.randint(len(far))]
    return np.exp2(a.ravel()).repeat(32)


def f64(x):
    return np.asarray(x).astype(np.float64)


def striped(idx):
    return np.tile(idx.reshape(-1, 16).T, (8, 1)).astype(np.uint16)


def unstriped(offs):
    return offs[:16].T.reshape(-1).astype(np.int64)


def pack_weight(w):
    k, n = w.shape
    w = f64(np.asarray(w, np.float32).astype(ml_dtypes.bfloat16)).reshape(k // 32, 32, n)
    amax = np.abs(w).max(1)
    byte = np.clip(np.where(amax > 0, np.frexp(amax)[1] - 1 + 127 - 7, 1), 1, 254)
    scaled = (w * np.exp2(127.0 - byte)[:, None, :]).reshape(k, n).astype(np.float32)
    words = np.ascontiguousarray(scaled.reshape(k // 512, 128, 4, n).transpose(0, 1, 3, 2)).astype(ml_dtypes.float8_e4m3fn).view(np.uint8)
    return words, np.ascontiguousarray(byte.astype(np.uint8).reshape(k // 512, 16, n))


def unpack_weight(words, scales):
    g, p, n, _ = words.shape
    vals = np.ascontiguousarray(words).view(ml_dtypes.float8_e4m3fn).astype(np.float64) * np.repeat(np.exp2(scales.astype(np.float64) - 127.0), 8, axis=1)[..., None]
    return vals.transpose(0, 1, 3, 2).reshape(g * 512, n)


K, T, S, N = 512, 2048, 512, 128
P = 2 ** 7


def setup_inputs():
    n = np.random.standard_normal
    s = mx_kscale(K)[:, None]
    packed_xT = pack_weight(n((K, T)) * s)
    return {
        "x_words": packed_xT[0],
        "x_scales": packed_xT[1],
        "w1": (n((K, N)) / np.sqrt(K) / s).astype(np.float32),
        "react": (np.random.uniform(0.0, 0.6, (N, S))).astype(np.float32),
        "res": (np.tile(np.random.uniform(0.02, 0.2, S), (P, 1))).astype(np.float32),
        "rea": (np.tile(np.random.uniform(0.02, 0.2, S), (P, 1))).astype(np.float32),
        "volt": (np.random.uniform(0.8, 1.2, (N, S))).astype(np.float32),
        "offs": striped(np.random.permutation(T)[:S]),
        "cha": striped(np.random.permutation(S)),
        "chb": striped(np.random.permutation(S)),
        "par": striped(np.random.randint(0, S, S)),
    }


def reference(x_words, x_scales, w1, react, res, rea, volt, offs, cha, chb, par):
    xq = unpack_weight(x_words, x_scales)[:, unstriped(offs)]
    y = mxq(f64(w1), 0, "e4m3").T @ xq
    load = np.log(np.exp(y) + 1.0)
    pf = load + 0.5 * (load[:, unstriped(cha)] + load[:, unstriped(chb)])
    qf = f64(react) + 0.5 * (f64(react)[:, unstriped(cha)] + f64(react)[:, unstriped(chb)])
    drop = 2.0 * (f64(res)[:1] * pf + f64(rea)[:1] * qf)
    va = f64(volt)[:, unstriped(par)] - drop
    return va[:, unstriped(par)] - drop

@@ -1,0 +1,156 @@
+from contextlib import ExitStack
+
+import concourse.mybir as mybir
+
+K, T, S, N = 512, 2048, 512, 128
+FLOPS = 2 * K * N * S
+
+F32 = mybir.dt.float32
+BF16 = mybir.dt.bfloat16
+I32 = mybir.dt.int32
+U32 = mybir.dt.uint32
+U16 = mybir.dt.uint16
+U8 = mybir.dt.uint8
+FP8X4 = mybir.dt.float8_e4m3fn_x4
+ALU = mybir.AluOpType
+ACT = mybir.ActivationFunctionType
+
+P = 128
+PACK = 4
+QUARTER = S // 4
+HALF = S // 2
+
+
+def entries(offsets, cols):
+    return offsets[:, cols.start // 16 : cols.stop // 16]
+
+
+def tile_picked_ylindst_volt_p_kernel(
+    tc, x_words, x_scales, w1, react, res, rea, volt, offs, cha, chb, par, out
+):
+    nc = tc.nc
+    quarters = [slice(c * QUARTER, (c + 1) * QUARTER) for c in range(4)]
+    first, second = slice(0, HALF), slice(HALF, S)
+
+    with ExitStack() as ctx:
+        sb = ctx.enter_context(tc.tile_pool(name="sb", bufs=1))
+        stage = ctx.enter_context(tc.tile_pool(name="stage", bufs=1))
+        psum = ctx.enter_context(tc.psum_pool(name="psum", bufs=1))
+
+        offs_sb = sb.tile([P, S // 16], U16)
+        cha_sb = sb.tile([P, S // 16], U16)
+        chb_sb = sb.tile([P, S // 16], U16)
+        par_sb = sb.tile([P, S // 16], U16)
+        words_sb = sb.tile([P, T], I32, align_bytes=64)
+        scales_sb = sb.tile([P, T], U8, align_bytes=64)
+        row = 4 * S
+        w_raw = stage.tile([P, PACK, N], F32, offset=row // 2)
+        w_grouped = stage.tile([P, N, PACK], BF16, align_bytes=64, offset=3 * row - row // 4)
+
+        nc.vector.memset(scales_sb[:].bitcast(I32), 0)
+        nc.sync.dma_start(offs_sb[:], offs)
+        nc.sync.dma_start(cha_sb[:], cha)
+        nc.sync.dma_start(out=w_raw[:], in_=w1.rearrange("(p j) m -> p j m", j=PACK))
+        nc.sync.dma_start(out=words_sb[:], in_=x_words[0].rearrange("p n t -> p (n t)").bitcast(I32))
+        nc.sync.dma_start(chb_sb[:], chb)
+        nc.sync.dma_start(par_sb[:], par)
+        for q in range(4):
+            nc.scalar.dma_start(
+                out=scales_sb[32 * q : 32 * q + 4, :].bitcast(I32),
+                in_=x_scales[0, 4 * q : 4 * q + 4, :].bitcast(I32),
+            )
+
+        w_codes = sb.tile([P, N], U32, align_bytes=64)
+        w_scales = sb.tile([P, N], U8, align_bytes=64)
+        nc.vector.tensor_copy(out=w_grouped[:], in_=w_raw[:].rearrange("p j m -> p m j"))
+        picked_scales = sb.tile([P, S], U8, align_bytes=64)
+        nc.vector.tensor_copy(picked_scales[:], scales_sb[:].indirect(offs_sb[:]))
+        nc.vector.quantize_mx(
+            out=w_codes[:].bitcast(FP8X4),
+            scales=w_scales[:],
+            in_=w_grouped[:].rearrange("p m j -> p (m j)"),
+        )
+
+        react_sb = stage.tile([P, S], F32, offset=0)
+        volt_sb = stage.tile([P, S], F32, offset=row)
+        rea_sb = stage.tile([P, S], F32, offset=2 * row)
+        res_sb = stage.tile([P, S], F32, offset=3 * row)
+        nc.sync.dma_start(out=react_sb[:], in_=react)
+        nc.sync.dma_start(out=rea_sb[:], in_=rea)
+        nc.sync.dma_start(out=volt_sb[:], in_=volt)
+        nc.sync.dma_start(out=res_sb[:], in_=res)
+
+        magnitude = sb.tile([P, S], F32, tag="magnitude")
+        decay = sb.tile([P, S], F32, tag="decay")
+        banks = []
+        for c, cols in enumerate(quarters):
+            picked_words = sb.tile([P, QUARTER], U32, align_bytes=64, name=f"picked_words{c}")
+            nc.vector.tensor_copy(picked_words[:], words_sb[:].bitcast(U32).indirect(entries(offs_sb, cols)))
+            y = psum.tile([P, QUARTER], F32, name=f"y{c}")
+            nc.tensor.matmul_mx(
+                out=y[:],
+                lhsT=w_codes[:].bitcast(FP8X4),
+                lhsT_scale=w_scales[:],
+                rhs=picked_words[:].bitcast(FP8X4),
+                rhs_scale=picked_scales[:, cols],
+                start=True,
+                stop=True,
+            )
+            banks.append(y)
+            nc.scalar.activation(magnitude[:, cols], y[:], ACT.Abs)
+            nc.scalar.activation(decay[:, cols], magnitude[:, cols], ACT.Exp, scale=-1.0)
+
+        react2 = sb.tile([P, S], F32)
+        qa = sb.tile([P, S], F32)
+        qb = sb.tile([P, S], F32)
+        q_drop = sb.tile([P, S], F32)
+        nc.vector.tensor_scalar(react2[:], react_sb[:], 2.0, None, ALU.mult)
+        for cols in (first, second):
+            nc.vector.tensor_tensor(qa[:, cols], react_sb[:].indirect(entries(cha_sb, cols)), react2[:, cols], ALU.add)
+        for cols in (first, second):
+            nc.vector.tensor_tensor(qb[:, cols], react_sb[:].indirect(entries(chb_sb, cols)), qa[:, cols], ALU.add)
+        for cols in (first, second):
+            nc.vector.tensor_tensor(q_drop[:, cols], qb[:, cols], rea_sb[:, cols], ALU.mult)
+
+        soft = sb.tile([P, S], F32, tag="magnitude")
+        load = sb.tile([P, S], F32)
+        for c, cols in enumerate(quarters):
+            nc.scalar.activation(soft[:, cols], decay[:, cols], ACT.Ln, bias=1.0)
+            nc.vector.scalar_tensor_tensor(load[:, cols], banks[c][:], 0.0, soft[:, cols], ALU.max, ALU.add)
+
+        volt_par_first = sb.tile([P, HALF], F32, tag="decay")
+        volt_par_second = sb.tile([P, HALF], F32, tag="magnitude")
+        load_a = sb.tile([P, HALF], F32)
+        load_b = sb.tile([P, S], F32)
+        load2 = sb.tile([P, HALF], F32)
+        partial = sb.tile([P, S], F32)
+        flow = sb.tile([P, S], F32)
+        p_drop = sb.tile([P, S], F32)
+        drop = sb.tile([P, S], F32)
+        va = sb.tile([P, S], F32)
+
+        nc.scalar.activation(volt_par_first[:], volt_sb[:].indirect(entries(par_sb, first)), ACT.Copy)
+        nc.scalar.activation(load_b[:, first], load[:].indirect(entries(chb_sb, first)), ACT.Copy)
+        nc.scalar.activation(load_a[:], load[:].indirect(entries(cha_sb, second)), ACT.Copy)
+        nc.scalar.activation(load_b[:, second], load[:].indirect(entries(chb_sb, second)), ACT.Copy)
+        nc.scalar.activation(volt_par_second[:], volt_sb[:].indirect(entries(par_sb, second)), ACT.Copy)
+
+        nc.vector.tensor_scalar(load2[:], load[:, first], 2.0, None, ALU.mult)
+        nc.vector.tensor_tensor(partial[:, first], load[:].indirect(entries(cha_sb, first)), load2[:], ALU.add)
+        nc.vector.tensor_tensor(flow[:, first], partial[:, first], load_b[:, first], ALU.add)
+        nc.vector.scalar_tensor_tensor(partial[:, second], load[:, second], 2.0, load_a[:], ALU.mult, ALU.add)
+        nc.vector.tensor_tensor(p_drop[:, first], flow[:, first], res_sb[:, first], ALU.mult)
+        nc.vector.tensor_tensor(flow[:, second], partial[:, second], load_b[:, second], ALU.add)
+        nc.vector.tensor_tensor(drop[:, first], p_drop[:, first], q_drop[:, first], ALU.add)
+        nc.vector.tensor_tensor(p_drop[:, second], flow[:, second], res_sb[:, second], ALU.mult)
+        nc.vector.tensor_tensor(va[:, first], volt_par_first[:], drop[:, first], ALU.subtract)
+        nc.vector.tensor_tensor(drop[:, second], p_drop[:, second], q_drop[:, second], ALU.add)
+        nc.vector.tensor_tensor(va[:, second], volt_par_second[:], drop[:, second], ALU.subtract)
+
+        va_par = sb.tile([P, HALF], F32)
+        result = sb.tile([P, S], F32)
+        nc.vector.tensor_tensor(result[:, first], va[:].indirect(entries(par_sb, first)), drop[:, first], ALU.subtract)
+        nc.scalar.activation(va_par[:], va[:].indirect(entries(par_sb, second)), ACT.Copy)
+        nc.sync.dma_start(out=out[:, first], in_=result[:, first])
+        nc.vector.tensor_tensor(result[:, second], va_par[:], drop[:, second], ALU.subtract)
+        nc.sync.dma_start(out=out[:, second], in_=result[:, second])

@@ -19,6 +19,7 @@ P = 128
 PACK = 4
 QUARTER = S // 4
 HALF = S // 2
+FUSED = 320
 
 
 def entries(offsets, cols):
@@ -34,7 +35,6 @@ def tile_picked_ylindst_volt_p_kernel(
 
     with ExitStack() as ctx:
         sb = ctx.enter_context(tc.tile_pool(name="sb", bufs=1))
-        stage = ctx.enter_context(tc.tile_pool(name="stage", bufs=1))
         psum = ctx.enter_context(tc.psum_pool(name="psum", bufs=1))
 
         offs_sb = sb.tile([P, S // 16], U16)
@@ -42,46 +42,46 @@ def tile_picked_ylindst_volt_p_kernel(
         chb_sb = sb.tile([P, S // 16], U16)
         par_sb = sb.tile([P, S // 16], U16)
         words_sb = sb.tile([P, T], I32, align_bytes=64)
+        scale_rows = sb.tile([P, T // 4], I32, align_bytes=64)
         scales_sb = sb.tile([P, T], U8, align_bytes=64)
-        row = 4 * S
-        w_raw = stage.tile([P, PACK, N], F32, offset=row // 2)
-        w_grouped = stage.tile([P, N, PACK], BF16, align_bytes=64, offset=3 * row - row // 4)
+        w_raw = sb.tile([P, PACK, N], F32)
+        react_sb = sb.tile([P, S], F32)
+        rea_sb = sb.tile([P, S], F32)
+        volt_sb = sb.tile([P, S], F32)
+        res_sb = sb.tile([P, S], F32)
 
-        nc.vector.memset(scales_sb[:].bitcast(I32), 0)
+        nc.scalar.dma_start(out=w_raw[:], in_=w1.rearrange("(p j) m -> p j m", j=PACK))
+        for q in range(4):
+            nc.sync.dma_start(out=scale_rows[32 * q : 32 * q + 4, :], in_=x_scales[0, 4 * q : 4 * q + 4, :].bitcast(I32))
         nc.sync.dma_start(offs_sb[:], offs)
-        nc.sync.dma_start(cha_sb[:], cha)
-        nc.sync.dma_start(out=w_raw[:], in_=w1.rearrange("(p j) m -> p j m", j=PACK))
         nc.sync.dma_start(out=words_sb[:], in_=x_words[0].rearrange("p n t -> p (n t)").bitcast(I32))
+        nc.sync.dma_start(out=react_sb[:], in_=react)
+        nc.sync.dma_start(cha_sb[:], cha)
         nc.sync.dma_start(chb_sb[:], chb)
         nc.sync.dma_start(par_sb[:], par)
-        for q in range(4):
-            nc.scalar.dma_start(
-                out=scales_sb[32 * q : 32 * q + 4, :].bitcast(I32),
-                in_=x_scales[0, 4 * q : 4 * q + 4, :].bitcast(I32),
-            )
+        nc.sync.dma_start(out=rea_sb[:], in_=rea)
+        nc.sync.dma_start(out=volt_sb[:], in_=volt)
+        nc.sync.dma_start(out=res_sb[:], in_=res)
 
-        w_codes = sb.tile([P, N], U32, align_bytes=64)
-        w_scales = sb.tile([P, N], U8, align_bytes=64)
-        nc.vector.tensor_copy(out=w_grouped[:], in_=w_raw[:].rearrange("p j m -> p m j"))
+        nc.vector.memset(scales_sb[:].bitcast(I32), 0)
+        for q in range(4):
+            rows = slice(32 * q, 32 * q + 4)
+            nc.vector.tensor_copy(scales_sb[rows, :].bitcast(I32), scale_rows[rows, :])
         picked_scales = sb.tile([P, S], U8, align_bytes=64)
         nc.vector.tensor_copy(picked_scales[:], scales_sb[:].indirect(offs_sb[:]))
+
+        w_grouped = sb.tile([P, N, PACK], BF16, align_bytes=64)
+        w_codes = sb.tile([P, N], U32, align_bytes=64)
+        w_scales = sb.tile([P, N], U8, align_bytes=64)
+        nc.scalar.activation(w_grouped[:], w_raw[:].rearrange("p j m -> p m j"), ACT.Copy)
         nc.vector.quantize_mx(
             out=w_codes[:].bitcast(FP8X4),
             scales=w_scales[:],
             in_=w_grouped[:].rearrange("p m j -> p (m j)"),
         )
 
-        react_sb = stage.tile([P, S], F32, offset=0)
-        volt_sb = stage.tile([P, S], F32, offset=row)
-        rea_sb = stage.tile([P, S], F32, offset=2 * row)
-        res_sb = stage.tile([P, S], F32, offset=3 * row)
-        nc.sync.dma_start(out=react_sb[:], in_=react)
-        nc.sync.dma_start(out=rea_sb[:], in_=rea)
-        nc.sync.dma_start(out=volt_sb[:], in_=volt)
-        nc.sync.dma_start(out=res_sb[:], in_=res)
-
         magnitude = sb.tile([P, S], F32, tag="magnitude")
-        decay = sb.tile([P, S], F32, tag="decay")
+        decay = sb.tile([P, S], F32)
         banks = []
         for c, cols in enumerate(quarters):
             picked_words = sb.tile([P, QUARTER], U32, align_bytes=64, name=f"picked_words{c}")
@@ -100,17 +100,14 @@ def tile_picked_ylindst_volt_p_kernel(
             nc.scalar.activation(magnitude[:, cols], y[:], ACT.Abs)
             nc.scalar.activation(decay[:, cols], magnitude[:, cols], ACT.Exp, scale=-1.0)
 
-        react2 = sb.tile([P, S], F32)
+        react2 = sb.tile([P, S], F32, align_bytes=64, tag="picked_words0")
         qa = sb.tile([P, S], F32)
         qb = sb.tile([P, S], F32)
-        q_drop = sb.tile([P, S], F32)
         nc.vector.tensor_scalar(react2[:], react_sb[:], 2.0, None, ALU.mult)
         for cols in (first, second):
             nc.vector.tensor_tensor(qa[:, cols], react_sb[:].indirect(entries(cha_sb, cols)), react2[:, cols], ALU.add)
         for cols in (first, second):
             nc.vector.tensor_tensor(qb[:, cols], react_sb[:].indirect(entries(chb_sb, cols)), qa[:, cols], ALU.add)
-        for cols in (first, second):
-            nc.vector.tensor_tensor(q_drop[:, cols], qb[:, cols], rea_sb[:, cols], ALU.mult)
 
         soft = sb.tile([P, S], F32, tag="magnitude")
         load = sb.tile([P, S], F32)
@@ -118,39 +115,41 @@ def tile_picked_ylindst_volt_p_kernel(
             nc.scalar.activation(soft[:, cols], decay[:, cols], ACT.Ln, bias=1.0)
             nc.vector.scalar_tensor_tensor(load[:, cols], banks[c][:], 0.0, soft[:, cols], ALU.max, ALU.add)
 
-        volt_par_first = sb.tile([P, HALF], F32, tag="decay")
-        volt_par_second = sb.tile([P, HALF], F32, tag="magnitude")
+        q_fall = sb.tile([P, S], F32, tag="magnitude")
         load_a = sb.tile([P, HALF], F32)
         load_b = sb.tile([P, S], F32)
-        load2 = sb.tile([P, HALF], F32)
+        load2 = sb.tile([P, HALF], F32, tag="load2")
         partial = sb.tile([P, S], F32)
         flow = sb.tile([P, S], F32)
-        p_drop = sb.tile([P, S], F32)
-        drop = sb.tile([P, S], F32)
+        p_fall = sb.tile([P, S], F32)
+        fall = sb.tile([P, S], F32)
         va = sb.tile([P, S], F32)
 
-        nc.scalar.activation(volt_par_first[:], volt_sb[:].indirect(entries(par_sb, first)), ACT.Copy)
         nc.scalar.activation(load_b[:, first], load[:].indirect(entries(chb_sb, first)), ACT.Copy)
         nc.scalar.activation(load_a[:], load[:].indirect(entries(cha_sb, second)), ACT.Copy)
         nc.scalar.activation(load_b[:, second], load[:].indirect(entries(chb_sb, second)), ACT.Copy)
-        nc.scalar.activation(volt_par_second[:], volt_sb[:].indirect(entries(par_sb, second)), ACT.Copy)
 
         nc.vector.tensor_scalar(load2[:], load[:, first], 2.0, None, ALU.mult)
         nc.vector.tensor_tensor(partial[:, first], load[:].indirect(entries(cha_sb, first)), load2[:], ALU.add)
+        volt_par = sb.tile([P, S], F32, tag="load2")
+        for cols in (first, second):
+            nc.scalar.activation(volt_par[:, cols], volt_sb[:].indirect(entries(par_sb, cols)), ACT.Copy)
+        nc.vector.scalar_tensor_tensor(q_fall[:], qb[:], -1.0, rea_sb[:], ALU.mult, ALU.mult)
         nc.vector.tensor_tensor(flow[:, first], partial[:, first], load_b[:, first], ALU.add)
         nc.vector.scalar_tensor_tensor(partial[:, second], load[:, second], 2.0, load_a[:], ALU.mult, ALU.add)
-        nc.vector.tensor_tensor(p_drop[:, first], flow[:, first], res_sb[:, first], ALU.mult)
+        nc.vector.scalar_tensor_tensor(p_fall[:, first], flow[:, first], -1.0, res_sb[:, first], ALU.mult, ALU.mult)
         nc.vector.tensor_tensor(flow[:, second], partial[:, second], load_b[:, second], ALU.add)
-        nc.vector.tensor_tensor(drop[:, first], p_drop[:, first], q_drop[:, first], ALU.add)
-        nc.vector.tensor_tensor(p_drop[:, second], flow[:, second], res_sb[:, second], ALU.mult)
-        nc.vector.tensor_tensor(va[:, first], volt_par_first[:], drop[:, first], ALU.subtract)
-        nc.vector.tensor_tensor(drop[:, second], p_drop[:, second], q_drop[:, second], ALU.add)
-        nc.vector.tensor_tensor(va[:, second], volt_par_second[:], drop[:, second], ALU.subtract)
+        nc.vector.tensor_tensor(fall[:, first], p_fall[:, first], q_fall[:, first], ALU.add)
+        nc.vector.scalar_tensor_tensor(p_fall[:, second], flow[:, second], -1.0, res_sb[:, second], ALU.mult, ALU.mult)
+        nc.vector.tensor_tensor(va[:, first], volt_par[:, first], fall[:, first], ALU.add)
+        nc.vector.tensor_tensor(fall[:, second], p_fall[:, second], q_fall[:, second], ALU.add)
+        nc.vector.tensor_tensor(va[:, second], volt_par[:, second], fall[:, second], ALU.add)
 
-        va_par = sb.tile([P, HALF], F32)
+        fused, apart = slice(0, FUSED), slice(FUSED, S)
+        va_par = sb.tile([P, S - FUSED], F32)
         result = sb.tile([P, S], F32)
-        nc.vector.tensor_tensor(result[:, first], va[:].indirect(entries(par_sb, first)), drop[:, first], ALU.subtract)
-        nc.scalar.activation(va_par[:], va[:].indirect(entries(par_sb, second)), ACT.Copy)
-        nc.sync.dma_start(out=out[:, first], in_=result[:, first])
-        nc.vector.tensor_tensor(result[:, second], va_par[:], drop[:, second], ALU.subtract)
-        nc.sync.dma_start(out=out[:, second], in_=result[:, second])
+        nc.vector.tensor_tensor(result[:, fused], va[:].indirect(entries(par_sb, fused)), fall[:, fused], ALU.add)
+        nc.scalar.activation(va_par[:], va[:].indirect(entries(par_sb, apart)), ACT.Copy)
+        nc.sync.dma_start(out=out[:, fused], in_=result[:, fused])
+        nc.vector.tensor_tensor(result[:, apart], va_par[:], fall[:, apart], ALU.add)
+        nc.sync.dma_start(out=out[:, apart], in_=result[:, apart])

from contextlib import ExitStack

import concourse.mybir as mybir

K, T, S, N = 512, 2048, 512, 128
FLOPS = 2 * K * N * S

F32 = mybir.dt.float32
BF16 = mybir.dt.bfloat16
I32 = mybir.dt.int32
U32 = mybir.dt.uint32
U16 = mybir.dt.uint16
U8 = mybir.dt.uint8
FP8X4 = mybir.dt.float8_e4m3fn_x4
ALU = mybir.AluOpType
ACT = mybir.ActivationFunctionType

P = 128
PACK = 4
QUARTER = S // 4
HALF = S // 2
FUSED = 320


def entries(offsets, cols):
    return offsets[:, cols.start // 16 : cols.stop // 16]


def tile_picked_ylindst_volt_p_kernel(
    tc, x_words, x_scales, w1, react, res, rea, volt, offs, cha, chb, par, out
):
    nc = tc.nc
    quarters = [slice(c * QUARTER, (c + 1) * QUARTER) for c in range(4)]
    first, second = slice(0, HALF), slice(HALF, S)

    with ExitStack() as ctx:
        sb = ctx.enter_context(tc.tile_pool(name="sb", bufs=1))
        psum = ctx.enter_context(tc.psum_pool(name="psum", bufs=1))

        offs_sb = sb.tile([P, S // 16], U16)
        cha_sb = sb.tile([P, S // 16], U16)
        chb_sb = sb.tile([P, S // 16], U16)
        par_sb = sb.tile([P, S // 16], U16)
        words_sb = sb.tile([P, T], I32, align_bytes=64)
        scale_rows = sb.tile([P, T // 4], I32, align_bytes=64)
        scales_sb = sb.tile([P, T], U8, align_bytes=64)
        w_raw = sb.tile([P, PACK, N], F32)
        react_sb = sb.tile([P, S], F32)
        rea_sb = sb.tile([P, S], F32)
        volt_sb = sb.tile([P, S], F32)
        res_sb = sb.tile([P, S], F32)

        nc.scalar.dma_start(out=w_raw[:], in_=w1.rearrange("(p j) m -> p j m", j=PACK))
        for q in range(4):
            nc.sync.dma_start(out=scale_rows[32 * q : 32 * q + 4, :], in_=x_scales[0, 4 * q : 4 * q + 4, :].bitcast(I32))
        nc.sync.dma_start(offs_sb[:], offs)
        nc.sync.dma_start(out=words_sb[:], in_=x_words[0].rearrange("p n t -> p (n t)").bitcast(I32))
        nc.sync.dma_start(out=react_sb[:], in_=react)
        nc.sync.dma_start(cha_sb[:], cha)
        nc.sync.dma_start(chb_sb[:], chb)
        nc.sync.dma_start(par_sb[:], par)
        nc.sync.dma_start(out=rea_sb[:], in_=rea)
        nc.sync.dma_start(out=volt_sb[:], in_=volt)
        nc.sync.dma_start(out=res_sb[:], in_=res)

        nc.vector.memset(scales_sb[:].bitcast(I32), 0)
        for q in range(4):
            rows = slice(32 * q, 32 * q + 4)
            nc.vector.tensor_copy(scales_sb[rows, :].bitcast(I32), scale_rows[rows, :])
        picked_scales = sb.tile([P, S], U8, align_bytes=64)
        nc.vector.tensor_copy(picked_scales[:], scales_sb[:].indirect(offs_sb[:]))

        w_grouped = sb.tile([P, N, PACK], BF16, align_bytes=64)
        w_codes = sb.tile([P, N], U32, align_bytes=64)
        w_scales = sb.tile([P, N], U8, align_bytes=64)
        nc.scalar.activation(w_grouped[:], w_raw[:].rearrange("p j m -> p m j"), ACT.Copy)
        nc.vector.quantize_mx(
            out=w_codes[:].bitcast(FP8X4),
            scales=w_scales[:],
            in_=w_grouped[:].rearrange("p m j -> p (m j)"),
        )

        magnitude = sb.tile([P, S], F32, tag="magnitude")
        decay = sb.tile([P, S], F32)
        banks = []
        for c, cols in enumerate(quarters):
            picked_words = sb.tile([P, QUARTER], U32, align_bytes=64, name=f"picked_words{c}")
            nc.vector.tensor_copy(picked_words[:], words_sb[:].bitcast(U32).indirect(entries(offs_sb, cols)))
            y = psum.tile([P, QUARTER], F32, name=f"y{c}")
            nc.tensor.matmul_mx(
                out=y[:],
                lhsT=w_codes[:].bitcast(FP8X4),
                lhsT_scale=w_scales[:],
                rhs=picked_words[:].bitcast(FP8X4),
                rhs_scale=picked_scales[:, cols],
                start=True,
                stop=True,
            )
            banks.append(y)
            nc.scalar.activation(magnitude[:, cols], y[:], ACT.Abs)
            nc.scalar.activation(decay[:, cols], magnitude[:, cols], ACT.Exp, scale=-1.0)

        react2 = sb.tile([P, S], F32, align_bytes=64, tag="picked_words0")
        qa = sb.tile([P, S], F32)
        qb = sb.tile([P, S], F32)
        nc.vector.tensor_scalar(react2[:], react_sb[:], 2.0, None, ALU.mult)
        for cols in (first, second):
            nc.vector.tensor_tensor(qa[:, cols], react_sb[:].indirect(entries(cha_sb, cols)), react2[:, cols], ALU.add)
        for cols in (first, second):
            nc.vector.tensor_tensor(qb[:, cols], react_sb[:].indirect(entries(chb_sb, cols)), qa[:, cols], ALU.add)

        soft = sb.tile([P, S], F32, tag="magnitude")
        load = sb.tile([P, S], F32)
        for c, cols in enumerate(quarters):
            nc.scalar.activation(soft[:, cols], decay[:, cols], ACT.Ln, bias=1.0)
            nc.vector.scalar_tensor_tensor(load[:, cols], banks[c][:], 0.0, soft[:, cols], ALU.max, ALU.add)

        q_fall = sb.tile([P, S], F32, tag="magnitude")
        load_a = sb.tile([P, HALF], F32)
        load_b = sb.tile([P, S], F32)
        load2 = sb.tile([P, HALF], F32, tag="load2")
        partial = sb.tile([P, S], F32)
        flow = sb.tile([P, S], F32)
        p_fall = sb.tile([P, S], F32)
        fall = sb.tile([P, S], F32)
        va = sb.tile([P, S], F32)

        nc.scalar.activation(load_b[:, first], load[:].indirect(entries(chb_sb, first)), ACT.Copy)
        nc.scalar.activation(load_a[:], load[:].indirect(entries(cha_sb, second)), ACT.Copy)
        nc.scalar.activation(load_b[:, second], load[:].indirect(entries(chb_sb, second)), ACT.Copy)

        nc.vector.tensor_scalar(load2[:], load[:, first], 2.0, None, ALU.mult)
        nc.vector.tensor_tensor(partial[:, first], load[:].indirect(entries(cha_sb, first)), load2[:], ALU.add)
        volt_par = sb.tile([P, S], F32, tag="load2")
        for cols in (first, second):
            nc.scalar.activation(volt_par[:, cols], volt_sb[:].indirect(entries(par_sb, cols)), ACT.Copy)
        nc.vector.scalar_tensor_tensor(q_fall[:], qb[:], -1.0, rea_sb[:], ALU.mult, ALU.mult)
        nc.vector.tensor_tensor(flow[:, first], partial[:, first], load_b[:, first], ALU.add)
        nc.vector.scalar_tensor_tensor(partial[:, second], load[:, second], 2.0, load_a[:], ALU.mult, ALU.add)
        nc.vector.scalar_tensor_tensor(p_fall[:, first], flow[:, first], -1.0, res_sb[:, first], ALU.mult, ALU.mult)
        nc.vector.tensor_tensor(flow[:, second], partial[:, second], load_b[:, second], ALU.add)
        nc.vector.tensor_tensor(fall[:, first], p_fall[:, first], q_fall[:, first], ALU.add)
        nc.vector.scalar_tensor_tensor(p_fall[:, second], flow[:, second], -1.0, res_sb[:, second], ALU.mult, ALU.mult)
        nc.vector.tensor_tensor(va[:, first], volt_par[:, first], fall[:, first], ALU.add)
        nc.vector.tensor_tensor(fall[:, second], p_fall[:, second], q_fall[:, second], ALU.add)
        nc.vector.tensor_tensor(va[:, second], volt_par[:, second], fall[:, second], ALU.add)

        fused, apart = slice(0, FUSED), slice(FUSED, S)
        va_par = sb.tile([P, S - FUSED], F32)
        result = sb.tile([P, S], F32)
        nc.vector.tensor_tensor(result[:, fused], va[:].indirect(entries(par_sb, fused)), fall[:, fused], ALU.add)
        nc.scalar.activation(va_par[:], va[:].indirect(entries(par_sb, apart)), ACT.Copy)
        nc.sync.dma_start(out=out[:, fused], in_=result[:, fused])
        nc.vector.tensor_tensor(result[:, apart], va_par[:], fall[:, apart], ALU.add)
        nc.sync.dma_start(out=out[:, apart], in_=result[:, apart])
